import numpy as np
import ml_dtypes


def mxq(x, axis, fmt="e4m3"):
    dtype, down = {"e4m3": (ml_dtypes.float8_e4m3fn, 7), "e5m2": (ml_dtypes.float8_e5m2, 14)}[fmt]
    v = np.moveaxis(np.asarray(x, np.float32).astype(ml_dtypes.bfloat16).astype(np.float64), axis, -1)
    blocks = v.reshape(v.shape[:-1] + (-1, 32))
    amax = np.abs(blocks).max(-1, keepdims=True)
    byte = np.maximum(np.where(amax > 0, np.frexp(amax)[1] - 1 + 127, 0) - down, 1)
    scale = np.exp2(byte - 127.0)
    codes = (blocks / scale).astype(np.float32).astype(dtype).astype(np.float64)
    return np.moveaxis((codes * scale).reshape(v.shape), -1, axis)


WIDE = False


def mx_kscale(k):
    if not WIDE:
        return np.ones(k)
    levels = np.array([10, -10, 5, -5, 0])
    if k % 512:
        return np.exp2(np.random.permutation(np.resize(levels, k // 32))).repeat(32)
    a = np.empty((k // 512, 16))
    for p in range(k // 512):
        a[p, :8] = np.random.permutation(np.resize(levels, 8))
        for g in range(8):
            far = levels[np.abs(levels - a[p, g]) >= 10]
            a[p, g + 8] = far[np.random.randint(len(far))]
    return np.exp2(a.ravel()).repeat(32)


def f64(x):
    return np.asarray(x).astype(np.float64)


def striped(idx):
    return np.tile(idx.reshape(-1, 16).T, (8, 1)).astype(np.uint16)


def unstriped(offs):
    return offs[:16].T.reshape(-1).astype(np.int64)


def pack_weight(w):
    k, n = w.shape
    w = f64(np.asarray(w, np.float32).astype(ml_dtypes.bfloat16)).reshape(k // 32, 32, n)
    amax = np.abs(w).max(1)
    byte = np.clip(np.where(amax > 0, np.frexp(amax)[1] - 1 + 127 - 7, 1), 1, 254)
    scaled = (w * np.exp2(127.0 - byte)[:, None, :]).reshape(k, n).astype(np.float32)
    words = np.ascontiguousarray(scaled.reshape(k // 512, 128, 4, n).transpose(0, 1, 3, 2)).astype(ml_dtypes.float8_e4m3fn).view(np.uint8)
    return words, np.ascontiguousarray(byte.astype(np.uint8).reshape(k // 512, 16, n))


def unpack_weight(words, scales):
    g, p, n, _ = words.shape
    vals = np.ascontiguousarray(words).view(ml_dtypes.float8_e4m3fn).astype(np.float64) * np.repeat(np.exp2(scales.astype(np.float64) - 127.0), 8, axis=1)[..., None]
    return vals.transpose(0, 1, 3, 2).reshape(g * 512, n)


E2M1 = np.array([0.0, 0.5, 1.0, 1.5, 2.0, 3.0, 4.0, 6.0, -0.0, -0.5, -1.0, -1.5, -2.0, -3.0, -4.0, -6.0])


def pack_fp4(w):
    k, n = w.shape
    w = f64(np.asarray(w, np.float32).astype(ml_dtypes.bfloat16)).reshape(k // 32, 32, n)
    amax = np.abs(w).max(1)
    mant, ex = np.frexp(amax / 6.0)
    byte = np.clip(np.where(amax > 0, np.where(mant > 0.5, ex, ex - 1) + 127, 1), 1, 254)
    scaled = (w * np.exp2(127.0 - byte)[:, None, :]).reshape(k, n).astype(np.float32)
    c = np.ascontiguousarray(scaled.reshape(k // 512, 128, 4, n).transpose(0, 1, 3, 2)).astype(ml_dtypes.float4_e2m1fn).view(np.uint8) & 0xF
    words = (c[..., 0::2] | (c[..., 1::2] << 4)).reshape(k // 512, 128, 2 * n)
    return np.ascontiguousarray(words), np.ascontiguousarray(byte.astype(np.uint8).reshape(k // 512, 16, n))


def unpack_fp4(words, scales):
    g, _, n = scales.shape
    words = np.ascontiguousarray(words).reshape(g, 128, n, 2)
    nib = np.empty((g, 128, n, 4), np.uint8)
    nib[..., 0::2] = words & 0xF
    nib[..., 1::2] = words >> 4
    vals = E2M1[nib] * np.repeat(np.exp2(scales.astype(np.float64) - 127.0), 8, axis=1)[..., None]
    return vals.transpose(0, 1, 3, 2).reshape(g * 512, n)


def planes(y):
    n, m = y.shape
    v = y.astype(np.float32).astype(ml_dtypes.bfloat16).astype(np.float64).reshape(n // 32, 32, m)
    top = np.abs(v).max(1)
    byte = np.clip(np.where(top > 0, np.frexp(top)[1] - 1 + 127 - 7, 1), 1, 254)
    codes = (v * np.exp2(127.0 - byte)[:, None, :]).reshape(n, m).astype(np.float32).astype(ml_dtypes.float8_e4m3fn).view(np.uint8)
    words = codes.reshape(n // 512, 128, 4, m).transpose(0, 1, 3, 2)
    return np.ascontiguousarray(words), np.ascontiguousarray(byte.astype(np.uint8).reshape(n // 512, 16, m))


K, T, S, N, H, U = 1024, 1024, 512, 512, 512, 1024


def setup_inputs():
    n = np.random.standard_normal
    s = mx_kscale(K)[:, None]
    u = mx_kscale(H)
    packed_xT = pack_weight(n((K, T)) * s)
    packed_w1 = pack_fp4(n((K, N)) / np.sqrt(K) / s)
    packed_w2 = pack_fp4(n((H, N)) / np.sqrt(H) / u[:, None])
    return {
        "x_words": packed_xT[0],
        "x_scales": packed_xT[1],
        "w1_words": packed_w1[0],
        "w1_scales": packed_w1[1],
        "unit": (np.random.uniform(0.6, 1.4, (H, 1)) * u[:, None]).astype(np.float32),
        "w2_words": packed_w2[0],
        "w2_scales": packed_w2[1],
        "offs": striped(np.random.permutation(T)[:S]),
        "s1": striped(np.random.permutation(np.concatenate([np.arange(S), np.random.randint(0, S, U - S)]))),
        "s2": striped(np.random.permutation(np.concatenate([np.arange(S), np.random.randint(0, S, U - S)]))),
        "s3": striped(np.random.permutation(np.concatenate([np.arange(S), np.random.randint(0, S, U - S)]))),
        "sk": striped(np.random.permutation(np.concatenate([np.arange(S), np.random.randint(0, S, U - S)]))),
    }


def reference(x_words, x_scales, w1_words, w1_scales, unit, w2_words, w2_scales, offs, s1, s2, s3, sk):
    xq = unpack_weight(x_words, x_scales)[:, unstriped(offs)]
    y = unpack_fp4(w1_words, w1_scales).T @ xq
    y1 = y[:, unstriped(s1)]
    y2 = y[:, unstriped(s2)]
    y3 = y[:, unstriped(s3)]
    path = y1 + y2 + y3
    yk = y[:, unstriped(sk)]
    hid = f64(unit) * np.maximum(path, 1.5 * yk)
    out_0 = unpack_fp4(w2_words, w2_scales).T @ mxq(hid, 0, "e4m3")
    return (out_0,) + planes(out_0)

@@ -1,0 +1,254 @@
+from contextlib import ExitStack
+
+import concourse.mybir as mybir
+
+K, T, S, N, H, U = 1024, 1024, 512, 512, 512, 1024
+FLOPS = 2 * K * N * S + 2 * H * N * U
+
+F32 = mybir.dt.float32
+BF16 = mybir.dt.bfloat16
+I32 = mybir.dt.int32
+U32 = mybir.dt.uint32
+U16 = mybir.dt.uint16
+U8 = mybir.dt.uint8
+FP8X4 = mybir.dt.float8_e4m3fn_x4
+FP4X4 = mybir.dt.float4_e2m1fn_x4
+ALU = mybir.AluOpType
+ACT = mybir.ActivationFunctionType
+
+P = 128
+PACK = 4
+PASSES = K // (P * PACK)
+STRIPE = 16
+BANK = 512
+SIGN_RUN = 64
+CHUNKS = (256, 256, 256, 128, 128)
+
+
+def tile_picked_yhopsum_max_po_kernel(
+    tc, x_words, x_scales, w1_words, w1_scales, unit, w2_words, w2_scales, offs, s1, s2, s3, sk, out_0, out_1, out_2
+):
+    nc = tc.nc
+    with ExitStack() as ctx:
+        keep = ctx.enter_context(tc.tile_pool(name="keep", bufs=1))
+        psum = ctx.enter_context(tc.psum_pool(name="psum", bufs=1))
+
+        def held(shape, dtype, name, tag=None):
+            return keep.tile(shape, dtype, name=name, tag=tag or name, align_bytes=64)
+
+        def load_scale_rows(dst, src):
+            for q in range(4):
+                nc.sync.dma_start(
+                    out=dst[32 * q : 32 * q + 4].bitcast(I32),
+                    in_=src[:, 4 * q : 4 * q + 4, :].rearrange("o r c -> r o c").bitcast(I32),
+                )
+
+        def load_list(src, name):
+            tile_ = keep.tile(list(src.shape), U16, name=name)
+            nc.sync.dma_start(tile_[:], src)
+            return tile_
+
+        xs_raw = held([P, PASSES, T], U8, "xs_raw")
+        w1s_raw = held([P, PASSES, N], U8, "w1s_raw")
+        w2s_raw = held([P, 1, N], U8, "w2s_raw")
+        nc.vector.memset(xs_raw[:].bitcast(I32), 0)
+        nc.gpsimd.memset(w1s_raw[:].bitcast(I32), 0)
+        nc.gpsimd.memset(w2s_raw[:].bitcast(I32), 0)
+
+        xw_raw = [held([P, T], U32, "xw_raw%d" % o) for o in range(PASSES)]
+
+        def load_x_words(o):
+            nc.sync.dma_start(out=xw_raw[o][:].bitcast(I32), in_=x_words[o].rearrange("p c r -> p (c r)").bitcast(I32))
+
+        load_x_words(0)
+        load_scale_rows(xs_raw, x_scales)
+        offs_t = load_list(offs, "offs_t")
+        w1w_raw = held([P, PASSES, 2 * N], U8, "w1w_raw")
+        nc.sync.dma_start(out=w1w_raw[:].bitcast(I32), in_=w1_words.rearrange("o p c -> p o c").bitcast(I32))
+        load_x_words(1)
+        load_scale_rows(w1s_raw, w1_scales)
+        unit_t = held([P, PACK], F32, "unit_t")
+        nc.sync.dma_start(out=unit_t[:], in_=unit.rearrange("(p t) o -> p (t o)", t=PACK))
+        s1_t = load_list(s1, "s1_t")
+        s2_t = load_list(s2, "s2_t")
+        s3_t = load_list(s3, "s3_t")
+        sk_t = load_list(sk, "sk_t")
+        w2w_raw = held([P, 1, 2 * N], U8, "w2w_raw")
+        nc.sync.dma_start(out=w2w_raw[:].bitcast(I32), in_=w2_words.rearrange("o p c -> p o c").bitcast(I32))
+        load_scale_rows(w2s_raw, w2_scales)
+
+        def deal_words(raw, passes, name):
+            dealt = held([P, passes, PACK, 2 * P], U8, name)
+            nc.vector.tensor_copy(
+                out=dealt[:].rearrange("p o t (m b) -> p o t m b", b=2),
+                in_=raw[:].rearrange("p o (m t b) -> p o t m b", t=PACK, b=2),
+            )
+            return dealt
+
+        def deal_scales(raw, passes, name):
+            dealt = held([P, passes, PACK, P], U8, name)
+            nc.vector.tensor_copy(out=dealt[:], in_=raw[:].rearrange("p o (m t) -> p o t m", t=PACK))
+            return dealt
+
+        xs = [held([P, S], U8, "xs%d" % o) for o in range(PASSES)]
+        xw = [held([P, S], U32, "xw%d" % o) for o in range(PASSES)]
+
+        def pick_columns(o):
+            nc.vector.tensor_copy(xw[o][:], xw_raw[o][:].indirect(offs_t[:]))
+            nc.vector.tensor_copy(xs[o][:], xs_raw[:, o, :].indirect(offs_t[:]))
+
+        pick_columns(0)
+        w1w = deal_words(w1w_raw, PASSES, "w1w")
+        w1s = deal_scales(w1s_raw, PASSES, "w1s")
+        pick_columns(1)
+
+        size = held([P, PACK], F32, "size")
+        nc.scalar.activation(size[:], unit_t[:], ACT.Abs)
+        sign = held([P, SIGN_RUN // PACK, PACK], BF16, "sign")
+        nc.scalar.activation(
+            sign[:], unit_t[:].unsqueeze(1).to_broadcast([P, SIGN_RUN // PACK, PACK]), ACT.Sign
+        )
+
+        y_banks = [psum.tile([P, S], F32, name="y_bank%d" % t) for t in range(PACK)]
+        for o in range(PASSES):
+            for t in range(PACK):
+                nc.tensor.matmul_mx(
+                    out=y_banks[t][:],
+                    lhsT=w1w[:, o, t, :].bitcast(FP4X4),
+                    lhsT_scale=w1s[:, o, t, :],
+                    rhs=xw[o][:].bitcast(FP8X4),
+                    rhs_scale=xs[o][:],
+                    start=(o == 0),
+                    stop=(o == PASSES - 1),
+                )
+        w2w = deal_words(w2w_raw, 1, "w2w")
+        y = []
+        for t in range(PACK):
+            rows = held([P, S], F32, "y%d" % t)
+            if t % 2 == 0:
+                nc.scalar.activation(rows[:], y_banks[t][:], ACT.Copy, scale=size[:, t : t + 1])
+            else:
+                nc.vector.tensor_scalar(rows[:], y_banks[t][:], size[:, t : t + 1], None, ALU.mult)
+            y.append(rows)
+        w2s = deal_scales(w2s_raw, 1, "w2s")
+
+        starts = [sum(CHUNKS[:c]) for c in range(len(CHUNKS))]
+        first, sink, hid, hid_words = {}, {}, {}, {}
+        second = [held([P, PACK, n], F32, "second%d" % c) for c, n in enumerate(CHUNKS)]
+        path = [held([P, PACK, n], F32, "path%d" % c) for c, n in enumerate(CHUNKS)]
+        larger = [held([P, PACK * n], BF16, "larger%d" % c) for c, n in enumerate(CHUNKS)]
+        hid_scales = [held([P, n], U8, "hid_scales%d" % c) for c, n in enumerate(CHUNKS)]
+        result = [held([P, PACK, n], F32, "result%d" % c) for c, n in enumerate(CHUNKS)]
+        rounded = [held([P, PACK * n], BF16, "rounded%d" % c) for c, n in enumerate(CHUNKS)]
+        out_words = held([P, U], U32, "out_words")
+        out_scales = held([P, U], U8, "out_scales")
+        out_rows = out_0.rearrange("(p t) r -> p t r", t=PACK)
+        out_words_hbm = out_1[0].rearrange("p c r -> p (c r)").bitcast(I32)
+
+        def entries(list_tile, c):
+            return list_tile[:, starts[c] // STRIPE : (starts[c] + CHUNKS[c]) // STRIPE]
+
+        def woven(flat):
+            return flat.rearrange("p (c i t) -> p c t i", i=2, t=PACK)
+
+        def planes(rows):
+            return rows.rearrange("p t (c i) -> p c t i", i=2)
+
+        def fetch_first(c, t):
+            if t == 0:
+                first[c] = held([P, PACK, CHUNKS[c]], F32, "first%d" % c, "hid_then_first%d" % c)
+            nc.scalar.activation(first[c][:, t, :], y[t][:].indirect(entries(s1_t, c)), ACT.Copy)
+
+        def fetch_sink(c, t):
+            if t == 0:
+                sink[c] = held([P, PACK, CHUNKS[c]], F32, "sink%d" % c, "words_then_sink%d" % c)
+            nc.scalar.activation(sink[c][:, t, :], y[t][:].indirect(entries(sk_t, c)), ACT.Copy, scale=1.5)
+
+        def add_second(c, t):
+            nc.vector.tensor_tensor(second[c][:, t, :], y[t][:].indirect(entries(s2_t, c)), first[c][:, t, :], ALU.add)
+
+        def add_third(c, t):
+            nc.vector.tensor_tensor(path[c][:, t, :], y[t][:].indirect(entries(s3_t, c)), second[c][:, t, :], ALU.add)
+
+        def take_larger(c):
+            nc.vector.tensor_tensor(woven(larger[c][:]), planes(path[c][:]), planes(sink[c][:]), ALU.max)
+
+        def give_sign(c):
+            runs = PACK * CHUNKS[c] // SIGN_RUN
+            hid[c] = held([P, PACK * CHUNKS[c]], BF16, "hid%d" % c, "hid_then_first%d" % (c + 2))
+            nc.vector.tensor_tensor(
+                hid[c][:].rearrange("p (a b) -> p a b", b=SIGN_RUN),
+                larger[c][:].rearrange("p (a b) -> p a b", b=SIGN_RUN),
+                sign[:].rearrange("p a t -> p (a t)").unsqueeze(1).to_broadcast([P, runs, SIGN_RUN]),
+                ALU.mult,
+            )
+
+        def multiply(c):
+            n = CHUNKS[c]
+            hid_words[c] = held([P, n], U32, "hid_words%d" % c, "words_then_sink%d" % (c + 2))
+            nc.vector.quantize_mx(out=hid_words[c][:].bitcast(FP8X4), scales=hid_scales[c][:], in_=hid[c][:])
+            per_bank = BANK // n
+            banks = []
+            for b in range(PACK // per_bank):
+                bank = psum.tile([P, per_bank, n], F32, name="out_bank", tag="out_bank", bufs=4)
+                for j in range(per_bank):
+                    t = b * per_bank + j
+                    nc.tensor.matmul_mx(
+                        out=bank[:, j, :],
+                        lhsT=w2w[:, 0, t, :].bitcast(FP4X4),
+                        lhsT_scale=w2s[:, 0, t, :],
+                        rhs=hid_words[c][:].bitcast(FP8X4),
+                        rhs_scale=hid_scales[c][:],
+                        start=True,
+                        stop=True,
+                    )
+                banks.append(bank)
+            return banks
+
+        def empty_banks(c, banks):
+            n = CHUNKS[c]
+            per_bank = BANK // n
+            for b, bank in enumerate(banks):
+                nc.scalar.copy(result[c][:, b * per_bank : (b + 1) * per_bank, :], bank[:])
+            nc.sync.dma_start(out=out_rows[:, :, starts[c] : starts[c] + n], in_=result[c][:])
+            if c == len(CHUNKS) - 1:
+                nc.vector.tensor_copy(woven(rounded[c][:]), planes(result[c][:]))
+            else:
+                nc.scalar.copy(woven(rounded[c][:]), planes(result[c][:]))
+
+        def hand_on(c):
+            cols = slice(starts[c], starts[c] + CHUNKS[c])
+            nc.vector.quantize_mx(out=out_words[:, cols].bitcast(FP8X4), scales=out_scales[:, cols], in_=rounded[c][:])
+            nc.sync.dma_start(out=out_words_hbm[:, cols], in_=out_words[:, cols].bitcast(I32))
+
+        last = len(CHUNKS) - 1
+        for c in range(last + 2):
+            if c <= last:
+                for t in range(PACK):
+                    fetch_first(c, t)
+                for t in range(PACK):
+                    fetch_sink(c, t)
+            banks = None
+            for t in range(PACK):
+                if c <= last:
+                    add_second(c, t)
+                if c >= 1:
+                    if t == 0:
+                        take_larger(c - 1)
+                    if t == 1:
+                        give_sign(c - 1)
+                    if t == 2:
+                        banks = multiply(c - 1)
+            if c >= 2:
+                hand_on(c - 2)
+            if c >= 1:
+                empty_banks(c - 1, banks)
+            if c <= last:
+                for t in range(PACK):
+                    add_third(c, t)
+        hand_on(last)
+        for q in range(4):
+            queue = nc.sync if q % 2 == 0 else nc.scalar
+            queue.dma_start(
+                out=out_2[0, 4 * q : 4 * q + 4, :].bitcast(I32), in_=out_scales[32 * q : 32 * q + 4, :].bitcast(I32)
+            )

@@ -22,7 +22,7 @@ PASSES = K // (P * PACK)
 STRIPE = 16
 BANK = 512
 SIGN_RUN = 64
-CHUNKS = (256, 256, 256, 128, 128)
+CHUNKS = (256, 384, 256, 128)
 
 
 def tile_picked_yhopsum_max_po_kernel(
@@ -36,9 +36,9 @@ def tile_picked_yhopsum_max_po_kernel(
         def held(shape, dtype, name, tag=None):
             return keep.tile(shape, dtype, name=name, tag=tag or name, align_bytes=64)
 
-        def load_scale_rows(dst, src):
+        def load_scale_rows(queue, dst, src):
             for q in range(4):
-                nc.sync.dma_start(
+                queue.dma_start(
                     out=dst[32 * q : 32 * q + 4].bitcast(I32),
                     in_=src[:, 4 * q : 4 * q + 4, :].rearrange("o r c -> r o c").bitcast(I32),
                 )
@@ -48,12 +48,12 @@ def tile_picked_yhopsum_max_po_kernel(
             nc.sync.dma_start(tile_[:], src)
             return tile_
 
-        xs_raw = held([P, PASSES, T], U8, "xs_raw")
+        xs_raw = held([P, T], U8, "xs_raw", "xs_then_w2w")
         w1s_raw = held([P, PASSES, N], U8, "w1s_raw")
-        w2s_raw = held([P, 1, N], U8, "w2s_raw")
+        xs_second = held([P, S], U8, "xs_second")
         nc.vector.memset(xs_raw[:].bitcast(I32), 0)
-        nc.gpsimd.memset(w1s_raw[:].bitcast(I32), 0)
-        nc.gpsimd.memset(w2s_raw[:].bitcast(I32), 0)
+        nc.vector.memset(w1s_raw[:].bitcast(I32), 0)
+        nc.vector.memset(xs_second[:].bitcast(I32), 0)
 
         xw_raw = [held([P, T], U32, "xw_raw%d" % o) for o in range(PASSES)]
 
@@ -61,46 +61,54 @@ def tile_picked_yhopsum_max_po_kernel(
             nc.sync.dma_start(out=xw_raw[o][:].bitcast(I32), in_=x_words[o].rearrange("p c r -> p (c r)").bitcast(I32))
 
         load_x_words(0)
-        load_scale_rows(xs_raw, x_scales)
+        for q in range(4):
+            nc.sync.dma_start(
+                out=xs_raw[32 * q : 32 * q + 4 * PASSES].bitcast(I32), in_=x_scales[:, 4 * q : 4 * q + 4, :].bitcast(I32)
+            )
         offs_t = load_list(offs, "offs_t")
         w1w_raw = held([P, PASSES, 2 * N], U8, "w1w_raw")
         nc.sync.dma_start(out=w1w_raw[:].bitcast(I32), in_=w1_words.rearrange("o p c -> p o c").bitcast(I32))
         load_x_words(1)
-        load_scale_rows(w1s_raw, w1_scales)
+        load_scale_rows(nc.sync, w1s_raw, w1_scales)
         unit_t = held([P, PACK], F32, "unit_t")
         nc.sync.dma_start(out=unit_t[:], in_=unit.rearrange("(p t) o -> p (t o)", t=PACK))
         s1_t = load_list(s1, "s1_t")
+        sk_t = load_list(sk, "sk_t")
         s2_t = load_list(s2, "s2_t")
         s3_t = load_list(s3, "s3_t")
-        sk_t = load_list(sk, "sk_t")
-        w2w_raw = held([P, 1, 2 * N], U8, "w2w_raw")
-        nc.sync.dma_start(out=w2w_raw[:].bitcast(I32), in_=w2_words.rearrange("o p c -> p o c").bitcast(I32))
-        load_scale_rows(w2s_raw, w2_scales)
 
-        def deal_words(raw, passes, name):
-            dealt = held([P, passes, PACK, 2 * P], U8, name)
+        def deal_words(dealt, raw):
             nc.vector.tensor_copy(
-                out=dealt[:].rearrange("p o t (m b) -> p o t m b", b=2),
-                in_=raw[:].rearrange("p o (m t b) -> p o t m b", t=PACK, b=2),
+                out=dealt.rearrange("p t (m b) -> p t m b", b=2),
+                in_=raw.rearrange("p (m t b) -> p t m b", t=PACK, b=2),
             )
-            return dealt
 
         def deal_scales(raw, passes, name):
             dealt = held([P, passes, PACK, P], U8, name)
             nc.vector.tensor_copy(out=dealt[:], in_=raw[:].rearrange("p o (m t) -> p o t m", t=PACK))
             return dealt
 
-        xs = [held([P, S], U8, "xs%d" % o) for o in range(PASSES)]
-        xw = [held([P, S], U32, "xw%d" % o) for o in range(PASSES)]
+        xs_first = held([P, S], U8, "xs_first")
+        nc.vector.tensor_copy(xs_first[:], xs_raw[:].indirect(offs_t[:]))
+        for q in range(4):
+            nc.scalar.dma_start(
+                out=xs_second[32 * q : 32 * q + 4].bitcast(I32), in_=xs_first[32 * q + 4 : 32 * q + 8].bitcast(I32)
+            )
+        xs = [xs_first, xs_second]
+        w2w_raw = held([P, 2 * N], U8, "w2w_raw", "xs_then_w2w")
+        nc.sync.dma_start(out=w2w_raw[:].bitcast(I32), in_=w2_words[0].bitcast(I32))
 
-        def pick_columns(o):
-            nc.vector.tensor_copy(xw[o][:], xw_raw[o][:].indirect(offs_t[:]))
-            nc.vector.tensor_copy(xs[o][:], xs_raw[:, o, :].indirect(offs_t[:]))
-
-        pick_columns(0)
-        w1w = deal_words(w1w_raw, PASSES, "w1w")
+        xw = [held([P, S], U32, "xw0")]
+        w1w = [held([P, PACK, 2 * P], U8, "w1w%d" % o) for o in range(PASSES)]
+        nc.vector.tensor_copy(xw[0][:], xw_raw[0][:].indirect(offs_t[:]))
+        deal_words(w1w[0][:], w1w_raw[:, 0, :])
+        deal_words(w1w[1][:], w1w_raw[:, 1, :])
         w1s = deal_scales(w1s_raw, PASSES, "w1s")
-        pick_columns(1)
+        xw.append(held([P, S], U32, "xw1", "w1s_raw"))
+        nc.vector.tensor_copy(xw[1][:], xw_raw[1][:].indirect(offs_t[:]))
+        w2s_raw = held([P, 1, N], U8, "w2s_raw", "w1w_raw")
+        nc.gpsimd.memset(w2s_raw[:].bitcast(I32), 0)
+        load_scale_rows(nc.sync, w2s_raw, w2_scales)
 
         size = held([P, PACK], F32, "size")
         nc.scalar.activation(size[:], unit_t[:], ACT.Abs)
@@ -110,33 +118,34 @@ def tile_picked_yhopsum_max_po_kernel(
         )
 
         y_banks = [psum.tile([P, S], F32, name="y_bank%d" % t) for t in range(PACK)]
-        for o in range(PASSES):
-            for t in range(PACK):
-                nc.tensor.matmul_mx(
-                    out=y_banks[t][:],
-                    lhsT=w1w[:, o, t, :].bitcast(FP4X4),
-                    lhsT_scale=w1s[:, o, t, :],
-                    rhs=xw[o][:].bitcast(FP8X4),
-                    rhs_scale=xs[o][:],
-                    start=(o == 0),
-                    stop=(o == PASSES - 1),
-                )
-        w2w = deal_words(w2w_raw, 1, "w2w")
-        y = []
-        for t in range(PACK):
-            rows = held([P, S], F32, "y%d" % t)
-            if t % 2 == 0:
-                nc.scalar.activation(rows[:], y_banks[t][:], ACT.Copy, scale=size[:, t : t + 1])
-            else:
-                nc.vector.tensor_scalar(rows[:], y_banks[t][:], size[:, t : t + 1], None, ALU.mult)
-            y.append(rows)
-        w2s = deal_scales(w2s_raw, 1, "w2s")
+        for pair in range(PACK // 2):
+            for o in range(PASSES):
+                for t in (2 * pair, 2 * pair + 1):
+                    nc.tensor.matmul_mx(
+                        out=y_banks[t][:],
+                        lhsT=w1w[o][:, t, :].bitcast(FP4X4),
+                        lhsT_scale=w1s[:, o, t, :],
+                        rhs=xw[o][:].bitcast(FP8X4),
+                        rhs_scale=xs[o][:],
+                        start=(o == 0),
+                        stop=(o == PASSES - 1),
+                    )
+        w2w = held([P, PACK, 2 * P], U8, "w2w")
+        deal_words(w2w[:], w2w_raw[:])
+        y = [held([P, S], F32, "y%d" % t) for t in range(PACK)]
 
+        def scale_rows(t):
+            if t % 2 == 0:
+                nc.scalar.activation(y[t][:], y_banks[t][:], ACT.Copy, scale=size[:, t : t + 1])
+            else:
+                nc.vector.tensor_scalar(y[t][:], y_banks[t][:], size[:, t : t + 1], None, ALU.mult)
+
+        last = len(CHUNKS) - 1
         starts = [sum(CHUNKS[:c]) for c in range(len(CHUNKS))]
-        first, sink, hid, hid_words = {}, {}, {}, {}
         second = [held([P, PACK, n], F32, "second%d" % c) for c, n in enumerate(CHUNKS)]
         path = [held([P, PACK, n], F32, "path%d" % c) for c, n in enumerate(CHUNKS)]
         larger = [held([P, PACK * n], BF16, "larger%d" % c) for c, n in enumerate(CHUNKS)]
+        hid = [held([P, PACK * n], BF16, "hid%d" % c) for c, n in enumerate(CHUNKS)]
         hid_scales = [held([P, n], U8, "hid_scales%d" % c) for c, n in enumerate(CHUNKS)]
         result = [held([P, PACK, n], F32, "result%d" % c) for c, n in enumerate(CHUNKS)]
         rounded = [held([P, PACK * n], BF16, "rounded%d" % c) for c, n in enumerate(CHUNKS)]
@@ -144,6 +153,9 @@ def tile_picked_yhopsum_max_po_kernel(
         out_scales = held([P, U], U8, "out_scales")
         out_rows = out_0.rearrange("(p t) r -> p t r", t=PACK)
         out_words_hbm = out_1[0].rearrange("p c r -> p (c r)").bitcast(I32)
+        first = {c: held([P, PACK, CHUNKS[c]], F32, "first%d" % c)[:] for c in range(last)}
+        sink = {c: held([P, PACK, CHUNKS[c]], F32, "sink%d" % c)[:] for c in range(last - 1)}
+        middle, hid_words, banks = {}, {}, {}
 
         def entries(list_tile, c):
             return list_tile[:, starts[c] // STRIPE : (starts[c] + CHUNKS[c]) // STRIPE]
@@ -155,27 +167,28 @@ def tile_picked_yhopsum_max_po_kernel(
             return rows.rearrange("p t (c i) -> p c t i", i=2)
 
         def fetch_first(c, t):
-            if t == 0:
-                first[c] = held([P, PACK, CHUNKS[c]], F32, "first%d" % c, "hid_then_first%d" % c)
-            nc.scalar.activation(first[c][:, t, :], y[t][:].indirect(entries(s1_t, c)), ACT.Copy)
+            if (c, t) == (0, 0):
+                nc.vector.tensor_copy(first[c][:, t, :], y[t][:].indirect(entries(s1_t, c)))
+            else:
+                nc.scalar.activation(first[c][:, t, :], y[t][:].indirect(entries(s1_t, c)), ACT.Copy)
+            if c == last:
+                nc.scalar.activation(middle[c][:, t, :], y[t][:].indirect(entries(s2_t, c)), ACT.Copy)
 
         def fetch_sink(c, t):
-            if t == 0:
-                sink[c] = held([P, PACK, CHUNKS[c]], F32, "sink%d" % c, "words_then_sink%d" % c)
             nc.scalar.activation(sink[c][:, t, :], y[t][:].indirect(entries(sk_t, c)), ACT.Copy, scale=1.5)
 
         def add_second(c, t):
-            nc.vector.tensor_tensor(second[c][:, t, :], y[t][:].indirect(entries(s2_t, c)), first[c][:, t, :], ALU.add)
+            other = middle[c][:, t, :] if c == last else y[t][:].indirect(entries(s2_t, c))
+            nc.vector.tensor_tensor(second[c][:, t, :], other, first[c][:, t, :], ALU.add)
 
         def add_third(c, t):
             nc.vector.tensor_tensor(path[c][:, t, :], y[t][:].indirect(entries(s3_t, c)), second[c][:, t, :], ALU.add)
 
         def take_larger(c):
-            nc.vector.tensor_tensor(woven(larger[c][:]), planes(path[c][:]), planes(sink[c][:]), ALU.max)
+            nc.vector.tensor_tensor(woven(larger[c][:]), planes(path[c][:]), planes(sink[c]), ALU.max)
 
         def give_sign(c):
             runs = PACK * CHUNKS[c] // SIGN_RUN
-            hid[c] = held([P, PACK * CHUNKS[c]], BF16, "hid%d" % c, "hid_then_first%d" % (c + 2))
             nc.vector.tensor_tensor(
                 hid[c][:].rearrange("p (a b) -> p a b", b=SIGN_RUN),
                 larger[c][:].rearrange("p (a b) -> p a b", b=SIGN_RUN),
@@ -183,35 +196,41 @@ def tile_picked_yhopsum_max_po_kernel(
                 ALU.mult,
             )
 
-        def multiply(c):
-            n = CHUNKS[c]
-            hid_words[c] = held([P, n], U32, "hid_words%d" % c, "words_then_sink%d" % (c + 2))
-            nc.vector.quantize_mx(out=hid_words[c][:].bitcast(FP8X4), scales=hid_scales[c][:], in_=hid[c][:])
-            per_bank = BANK // n
-            banks = []
-            for b in range(PACK // per_bank):
-                bank = psum.tile([P, per_bank, n], F32, name="out_bank", tag="out_bank", bufs=4)
-                for j in range(per_bank):
-                    t = b * per_bank + j
-                    nc.tensor.matmul_mx(
-                        out=bank[:, j, :],
-                        lhsT=w2w[:, 0, t, :].bitcast(FP4X4),
-                        lhsT_scale=w2s[:, 0, t, :],
-                        rhs=hid_words[c][:].bitcast(FP8X4),
-                        rhs_scale=hid_scales[c][:],
-                        start=True,
-                        stop=True,
-                    )
-                banks.append(bank)
-            return banks
+        def blocks(c):
+            found, at = [], 0
+            while at < CHUNKS[c]:
+                width = 2 * P if CHUNKS[c] - at >= 2 * P else P
+                found.append((at, width))
+                at = at + width
+            return found
 
-        def empty_banks(c, banks):
-            n = CHUNKS[c]
-            per_bank = BANK // n
-            for b, bank in enumerate(banks):
-                nc.scalar.copy(result[c][:, b * per_bank : (b + 1) * per_bank, :], bank[:])
-            nc.sync.dma_start(out=out_rows[:, :, starts[c] : starts[c] + n], in_=result[c][:])
-            if c == len(CHUNKS) - 1:
+        def multiply(c):
+            hid_words[c] = held([P, CHUNKS[c]], U32, "hid_words%d" % c)
+            nc.vector.quantize_mx(out=hid_words[c][:].bitcast(FP8X4), scales=hid_scales[c][:], in_=hid[c][:])
+            banks[c] = []
+            for at, width in blocks(c):
+                per_bank = BANK // width
+                for t0 in range(0, PACK, per_bank):
+                    bank = psum.tile([P, per_bank, width], F32, name="out_bank", tag="out_bank", bufs=4)
+                    for j in range(per_bank):
+                        nc.tensor.matmul_mx(
+                            out=bank[:, j, :],
+                            lhsT=w2w[:, t0 + j, :].bitcast(FP4X4),
+                            lhsT_scale=w2s[:, 0, t0 + j, :],
+                            rhs=hid_words[c][:, at : at + width].bitcast(FP8X4),
+                            rhs_scale=hid_scales[c][:, at : at + width],
+                            start=True,
+                            stop=True,
+                        )
+                    banks[c].append((bank, result[c][:, t0 : t0 + per_bank, at : at + width]))
+
+        def empty_banks(c):
+            for bank, place in banks[c]:
+                nc.scalar.copy(place, bank[:])
+            nc.sync.dma_start(out=out_rows[:, :, starts[c] : starts[c] + CHUNKS[c]], in_=result[c][:])
+
+        def round_result(c):
+            if c >= last - 1:
                 nc.vector.tensor_copy(woven(rounded[c][:]), planes(result[c][:]))
             else:
                 nc.scalar.copy(woven(rounded[c][:]), planes(result[c][:]))
@@ -221,32 +240,71 @@ def tile_picked_yhopsum_max_po_kernel(
             nc.vector.quantize_mx(out=out_words[:, cols].bitcast(FP8X4), scales=out_scales[:, cols], in_=rounded[c][:])
             nc.sync.dma_start(out=out_words_hbm[:, cols], in_=out_words[:, cols].bitcast(I32))
 
-        last = len(CHUNKS) - 1
-        for c in range(last + 2):
-            if c <= last:
-                for t in range(PACK):
-                    fetch_first(c, t)
-                for t in range(PACK):
-                    fetch_sink(c, t)
-            banks = None
-            for t in range(PACK):
-                if c <= last:
-                    add_second(c, t)
-                if c >= 1:
-                    if t == 0:
-                        take_larger(c - 1)
-                    if t == 1:
-                        give_sign(c - 1)
-                    if t == 2:
-                        banks = multiply(c - 1)
-            if c >= 2:
-                hand_on(c - 2)
-            if c >= 1:
-                empty_banks(c - 1, banks)
-            if c <= last:
-                for t in range(PACK):
-                    add_third(c, t)
-        hand_on(last)
+        def hidden_steps(c):
+            return [lambda: take_larger(c), lambda: give_sign(c), lambda: multiply(c), lambda: None]
+
+        scale_rows(0)
+        fetch_first(0, 0)
+        fetch_sink(0, 0)
+        scale_rows(1)
+        scale_rows(2)
+        add_second(0, 0)
+        scale_rows(3)
+        for t in range(1, PACK):
+            fetch_first(0, t)
+            add_second(0, t)
+        for t in range(1, PACK):
+            fetch_sink(0, t)
+        w2s = deal_scales(w2s_raw, 1, "w2s")
+        for t in range(PACK):
+            add_third(0, t)
+        for t in range(PACK):
+            fetch_first(1, t)
+        for t in range(PACK):
+            fetch_sink(1, t)
+        for t in range(PACK):
+            fetch_first(2, t)
+        for t, step in enumerate(hidden_steps(0)):
+            add_second(1, t)
+            step()
+        empty_banks(0)
+        round_result(0)
+        late = held([P, PACK * (CHUNKS[last - 1] + 3 * CHUNKS[last])], F32, "late", "hid_words0")
+        at = 0
+        for table, c in ((sink, last - 1), (first, last), (middle, last), (sink, last)):
+            table[c] = late[:, at : at + PACK * CHUNKS[c]].rearrange("p (t r) -> p t r", t=PACK)
+            at = at + PACK * CHUNKS[c]
+        for t in range(PACK):
+            fetch_sink(2, t)
+        for t in range(PACK):
+            fetch_first(3, t)
+        for t in range(PACK):
+            fetch_sink(3, t)
+        for t in range(PACK):
+            add_third(1, t)
+        for t, step in enumerate(hidden_steps(1)):
+            add_second(2, t)
+            step()
+        empty_banks(1)
+        round_result(1)
+        for t in range(PACK):
+            add_third(2, t)
+        for t, step in enumerate(hidden_steps(2)):
+            add_second(3, t)
+            step()
+        empty_banks(2)
+        for t in range(PACK):
+            add_third(3, t)
+        take_larger(3)
+        hand_on(0)
+        give_sign(3)
+        multiply(3)
+        empty_banks(3)
+        hand_on(1)
+        round_result(2)
+        hand_on(2)
+        round_result(3)
+        hand_on(3)
         for q in range(4):
             queue = nc.sync if q % 2 == 0 else nc.scalar
             queue.dma_start(

@@ -60,16 +60,16 @@ def tile_picked_yhopsum_max_po_kernel(
         def load_x_words(o):
             nc.sync.dma_start(out=xw_raw[o][:].bitcast(I32), in_=x_words[o].rearrange("p c r -> p (c r)").bitcast(I32))
 
-        load_x_words(0)
+        w1w_raw = held([P, PASSES, 2 * N], U8, "w1w_raw")
+        nc.sync.dma_start(out=w1w_raw[:].bitcast(I32), in_=w1_words.rearrange("o p c -> p o c").bitcast(I32))
         for q in range(4):
             nc.sync.dma_start(
                 out=xs_raw[32 * q : 32 * q + 4 * PASSES].bitcast(I32), in_=x_scales[:, 4 * q : 4 * q + 4, :].bitcast(I32)
             )
         offs_t = load_list(offs, "offs_t")
-        w1w_raw = held([P, PASSES, 2 * N], U8, "w1w_raw")
-        nc.sync.dma_start(out=w1w_raw[:].bitcast(I32), in_=w1_words.rearrange("o p c -> p o c").bitcast(I32))
-        load_x_words(1)
+        load_x_words(0)
         load_scale_rows(nc.sync, w1s_raw, w1_scales)
+        load_x_words(1)
         unit_t = held([P, PACK], F32, "unit_t")
         nc.sync.dma_start(out=unit_t[:], in_=unit.rearrange("(p t) o -> p (t o)", t=PACK))
         s1_t = load_list(s1, "s1_t")
@@ -99,14 +99,18 @@ def tile_picked_yhopsum_max_po_kernel(
         nc.sync.dma_start(out=w2w_raw[:].bitcast(I32), in_=w2_words[0].bitcast(I32))
 
         xw = [held([P, S], U32, "xw0")]
-        w1w = [held([P, PACK, 2 * P], U8, "w1w%d" % o) for o in range(PASSES)]
-        nc.vector.tensor_copy(xw[0][:], xw_raw[0][:].indirect(offs_t[:]))
+        w1w = [held([P, PACK, 2 * P], U8, "w1w0")]
         deal_words(w1w[0][:], w1w_raw[:, 0, :])
-        deal_words(w1w[1][:], w1w_raw[:, 1, :])
+        nc.vector.tensor_copy(xw[0][:], xw_raw[0][:].indirect(offs_t[:]))
         w1s = deal_scales(w1s_raw, PASSES, "w1s")
-        xw.append(held([P, S], U32, "xw1", "w1s_raw"))
-        nc.vector.tensor_copy(xw[1][:], xw_raw[1][:].indirect(offs_t[:]))
-        w2s_raw = held([P, 1, N], U8, "w2s_raw", "w1w_raw")
+        w1w.append(held([P, PACK, 2 * P], U8, "w1w1", "w1s_raw"))
+        deal_words(w1w[1][:], w1w_raw[:, 1, :])
+        xw.append(held([P, S], U32, "xw1", "w1w_raw"))
+        halves = [slice(h * S // 2, (h + 1) * S // 2) for h in range(2)]
+        for cols in halves:
+            picks = offs_t[:, cols.start // STRIPE : cols.stop // STRIPE]
+            nc.vector.tensor_copy(xw[1][:, cols], xw_raw[1][:].indirect(picks))
+        w2s_raw = held([P, 1, N], U8, "w2s_raw", "xw_raw0")
         nc.gpsimd.memset(w2s_raw[:].bitcast(I32), 0)
         load_scale_rows(nc.sync, w2s_raw, w2_scales)
 
@@ -117,28 +121,35 @@ def tile_picked_yhopsum_max_po_kernel(
             sign[:], unit_t[:].unsqueeze(1).to_broadcast([P, SIGN_RUN // PACK, PACK]), ACT.Sign
         )
 
-        y_banks = [psum.tile([P, S], F32, name="y_bank%d" % t) for t in range(PACK)]
+        def new_bank(shape):
+            return psum.tile(shape, F32, name="bank", tag="bank", bufs=8)
+
+        spans = [halves] + [[slice(0, S)]] * (PACK - 1)
+        y_banks = [[new_bank([P, cols.stop - cols.start]) for cols in spans[t]] for t in range(PACK)]
+
+        def first_product(t, o):
+            for bank, cols in zip(y_banks[t], spans[t]):
+                nc.tensor.matmul_mx(
+                    out=bank[:],
+                    lhsT=w1w[o][:, t, :].bitcast(FP4X4),
+                    lhsT_scale=w1s[:, o, t, :],
+                    rhs=xw[o][:, cols].bitcast(FP8X4),
+                    rhs_scale=xs[o][:, cols],
+                    start=(o == 0),
+                    stop=(o == PASSES - 1),
+                )
+
         for pair in range(PACK // 2):
             for o in range(PASSES):
                 for t in (2 * pair, 2 * pair + 1):
-                    nc.tensor.matmul_mx(
-                        out=y_banks[t][:],
-                        lhsT=w1w[o][:, t, :].bitcast(FP4X4),
-                        lhsT_scale=w1s[:, o, t, :],
-                        rhs=xw[o][:].bitcast(FP8X4),
-                        rhs_scale=xs[o][:],
-                        start=(o == 0),
-                        stop=(o == PASSES - 1),
-                    )
+                    first_product(t, o)
         w2w = held([P, PACK, 2 * P], U8, "w2w")
         deal_words(w2w[:], w2w_raw[:])
         y = [held([P, S], F32, "y%d" % t) for t in range(PACK)]
 
         def scale_rows(t):
-            if t % 2 == 0:
-                nc.scalar.activation(y[t][:], y_banks[t][:], ACT.Copy, scale=size[:, t : t + 1])
-            else:
-                nc.vector.tensor_scalar(y[t][:], y_banks[t][:], size[:, t : t + 1], None, ALU.mult)
+            for bank, cols in zip(y_banks[t], spans[t]):
+                nc.scalar.activation(y[t][:, cols], bank[:], ACT.Copy, scale=size[:, t : t + 1])
 
         last = len(CHUNKS) - 1
         starts = [sum(CHUNKS[:c]) for c in range(len(CHUNKS))]
@@ -148,8 +159,7 @@ def tile_picked_yhopsum_max_po_kernel(
         hid = [held([P, PACK * n], BF16, "hid%d" % c) for c, n in enumerate(CHUNKS)]
         hid_scales = [held([P, n], U8, "hid_scales%d" % c) for c, n in enumerate(CHUNKS)]
         result = [held([P, PACK, n], F32, "result%d" % c) for c, n in enumerate(CHUNKS)]
-        rounded = [held([P, PACK * n], BF16, "rounded%d" % c) for c, n in enumerate(CHUNKS)]
-        out_words = held([P, U], U32, "out_words")
+        rounded = {}
         out_scales = held([P, U], U8, "out_scales")
         out_rows = out_0.rearrange("(p t) r -> p t r", t=PACK)
         out_words_hbm = out_1[0].rearrange("p c r -> p (c r)").bitcast(I32)
@@ -167,18 +177,22 @@ def tile_picked_yhopsum_max_po_kernel(
             return rows.rearrange("p t (c i) -> p c t i", i=2)
 
         def fetch_first(c, t):
-            if (c, t) == (0, 0):
+            if c == 0 and t < 2:
                 nc.vector.tensor_copy(first[c][:, t, :], y[t][:].indirect(entries(s1_t, c)))
             else:
                 nc.scalar.activation(first[c][:, t, :], y[t][:].indirect(entries(s1_t, c)), ACT.Copy)
-            if c == last:
-                nc.scalar.activation(middle[c][:, t, :], y[t][:].indirect(entries(s2_t, c)), ACT.Copy)
+
+        def scalar_fetches_second(c, t):
+            return c == last or (c, t) == (last - 1, PACK - 1)
+
+        def fetch_second(c, t):
+            nc.scalar.activation(middle[c, t], y[t][:].indirect(entries(s2_t, c)), ACT.Copy)
 
         def fetch_sink(c, t):
             nc.scalar.activation(sink[c][:, t, :], y[t][:].indirect(entries(sk_t, c)), ACT.Copy, scale=1.5)
 
         def add_second(c, t):
-            other = middle[c][:, t, :] if c == last else y[t][:].indirect(entries(s2_t, c))
+            other = middle[c, t] if scalar_fetches_second(c, t) else y[t][:].indirect(entries(s2_t, c))
             nc.vector.tensor_tensor(second[c][:, t, :], other, first[c][:, t, :], ALU.add)
 
         def add_third(c, t):
@@ -209,9 +223,9 @@ def tile_picked_yhopsum_max_po_kernel(
             nc.vector.quantize_mx(out=hid_words[c][:].bitcast(FP8X4), scales=hid_scales[c][:], in_=hid[c][:])
             banks[c] = []
             for at, width in blocks(c):
-                per_bank = BANK // width
+                per_bank = 2 if c == last else BANK // width
                 for t0 in range(0, PACK, per_bank):
-                    bank = psum.tile([P, per_bank, width], F32, name="out_bank", tag="out_bank", bufs=4)
+                    bank = new_bank([P, per_bank, width])
                     for j in range(per_bank):
                         nc.tensor.matmul_mx(
                             out=bank[:, j, :],
@@ -230,6 +244,7 @@ def tile_picked_yhopsum_max_po_kernel(
             nc.sync.dma_start(out=out_rows[:, :, starts[c] : starts[c] + CHUNKS[c]], in_=result[c][:])
 
         def round_result(c):
+            rounded[c] = held([P, PACK * CHUNKS[c]], BF16, "rounded%d" % c, "rounded1" if c == last - 1 else None)
             if c >= last - 1:
                 nc.vector.tensor_copy(woven(rounded[c][:]), planes(result[c][:]))
             else:
@@ -237,27 +252,23 @@ def tile_picked_yhopsum_max_po_kernel(
 
         def hand_on(c):
             cols = slice(starts[c], starts[c] + CHUNKS[c])
-            nc.vector.quantize_mx(out=out_words[:, cols].bitcast(FP8X4), scales=out_scales[:, cols], in_=rounded[c][:])
-            nc.sync.dma_start(out=out_words_hbm[:, cols], in_=out_words[:, cols].bitcast(I32))
+            out_words = held([P, CHUNKS[c]], U32, "out_words%d" % c, {0: "path3", 1: "hid3"}.get(c))
+            nc.vector.quantize_mx(out=out_words[:].bitcast(FP8X4), scales=out_scales[:, cols], in_=rounded[c][:])
+            nc.sync.dma_start(out=out_words_hbm[:, cols], in_=out_words[:].bitcast(I32))
 
         def hidden_steps(c):
             return [lambda: take_larger(c), lambda: give_sign(c), lambda: multiply(c), lambda: None]
 
-        scale_rows(0)
-        fetch_first(0, 0)
-        fetch_sink(0, 0)
-        scale_rows(1)
-        scale_rows(2)
-        add_second(0, 0)
-        scale_rows(3)
-        for t in range(1, PACK):
+        for t in range(PACK):
+            scale_rows(t)
             fetch_first(0, t)
+            if t >= 1:
+                add_third(0, t - 1)
             add_second(0, t)
-        for t in range(1, PACK):
+        for t in range(PACK):
             fetch_sink(0, t)
         w2s = deal_scales(w2s_raw, 1, "w2s")
-        for t in range(PACK):
-            add_third(0, t)
+        add_third(0, PACK - 1)
         for t in range(PACK):
             fetch_first(1, t)
         for t in range(PACK):
@@ -269,15 +280,21 @@ def tile_picked_yhopsum_max_po_kernel(
             step()
         empty_banks(0)
         round_result(0)
-        late = held([P, PACK * (CHUNKS[last - 1] + 3 * CHUNKS[last])], F32, "late", "hid_words0")
-        at = 0
-        for table, c in ((sink, last - 1), (first, last), (middle, last), (sink, last)):
+        wide, narrow = CHUNKS[last - 1], CHUNKS[last]
+        late = held([P, (PACK + 1) * wide + 3 * PACK * narrow], F32, "late", "hid_words0")
+        middle[last - 1, PACK - 1] = late[:, :wide]
+        at = wide
+        for table, c in ((sink, last - 1), (first, last), (sink, last)):
             table[c] = late[:, at : at + PACK * CHUNKS[c]].rearrange("p (t r) -> p t r", t=PACK)
             at = at + PACK * CHUNKS[c]
+        for t in range(PACK):
+            middle[last, t] = late[:, at + t * narrow : at + (t + 1) * narrow]
+        fetch_second(2, PACK - 1)
         for t in range(PACK):
             fetch_sink(2, t)
         for t in range(PACK):
             fetch_first(3, t)
+            fetch_second(3, t)
         for t in range(PACK):
             fetch_sink(3, t)
         for t in range(PACK):

@@ -23,6 +23,8 @@ STRIPE = 16
 BANK = 512
 SIGN_RUN = 64
 CHUNKS = (256, 384, 256, 128)
+STORE_GROUPS = ((0,), (1, 2), (3,))
+SHARED_FROM = 2
 
 
 def tile_picked_yhopsum_max_po_kernel(
@@ -95,8 +97,12 @@ def tile_picked_yhopsum_max_po_kernel(
                 out=xs_second[32 * q : 32 * q + 4].bitcast(I32), in_=xs_first[32 * q + 4 : 32 * q + 8].bitcast(I32)
             )
         xs = [xs_first, xs_second]
-        w2w_raw = held([P, 2 * N], U8, "w2w_raw", "xs_then_w2w")
-        nc.sync.dma_start(out=w2w_raw[:].bitcast(I32), in_=w2_words[0].bitcast(I32))
+        w2_raw = held([P, 3, N], U8, "w2_raw", "xs_then_w2w")
+        w2w_raw = w2_raw[:, 0:2, :].rearrange("p a c -> p (a c)")
+        w2s_raw = w2_raw[:, 2:3, :]
+        nc.sync.dma_start(out=w2w_raw.bitcast(I32), in_=w2_words[0].bitcast(I32))
+        nc.gpsimd.memset(w2s_raw.bitcast(I32), 0)
+        load_scale_rows(nc.sync, w2s_raw, w2_scales)
 
         xw = [held([P, S], U32, "xw0")]
         w1w = [held([P, PACK, 2 * P], U8, "w1w0")]
@@ -110,9 +116,6 @@ def tile_picked_yhopsum_max_po_kernel(
         for cols in halves:
             picks = offs_t[:, cols.start // STRIPE : cols.stop // STRIPE]
             nc.vector.tensor_copy(xw[1][:, cols], xw_raw[1][:].indirect(picks))
-        w2s_raw = held([P, 1, N], U8, "w2s_raw", "xw_raw0")
-        nc.gpsimd.memset(w2s_raw[:].bitcast(I32), 0)
-        load_scale_rows(nc.sync, w2s_raw, w2_scales)
 
         size = held([P, PACK], F32, "size")
         nc.scalar.activation(size[:], unit_t[:], ACT.Abs)
@@ -144,7 +147,8 @@ def tile_picked_yhopsum_max_po_kernel(
                 for t in (2 * pair, 2 * pair + 1):
                     first_product(t, o)
         w2w = held([P, PACK, 2 * P], U8, "w2w")
-        deal_words(w2w[:], w2w_raw[:])
+        deal_words(w2w[:], w2w_raw)
+        w2s = deal_scales(w2s_raw, 1, "w2s")
         y = [held([P, S], F32, "y%d" % t) for t in range(PACK)]
 
         def scale_rows(t):
@@ -159,7 +163,7 @@ def tile_picked_yhopsum_max_po_kernel(
         hid = [held([P, PACK * n], BF16, "hid%d" % c) for c, n in enumerate(CHUNKS)]
         hid_scales = [held([P, n], U8, "hid_scales%d" % c) for c, n in enumerate(CHUNKS)]
         result = [held([P, PACK, n], F32, "result%d" % c) for c, n in enumerate(CHUNKS)]
-        rounded = {}
+        rounded, out_words = {}, {}
         out_scales = held([P, U], U8, "out_scales")
         out_rows = out_0.rearrange("(p t) r -> p t r", t=PACK)
         out_words_hbm = out_1[0].rearrange("p c r -> p (c r)").bitcast(I32)
@@ -171,10 +175,10 @@ def tile_picked_yhopsum_max_po_kernel(
             return list_tile[:, starts[c] // STRIPE : (starts[c] + CHUNKS[c]) // STRIPE]
 
         def woven(flat):
-            return flat.rearrange("p (c i t) -> p c t i", i=2, t=PACK)
+            return flat.rearrange("p (c i t) -> p c t i", i=4, t=PACK)
 
         def planes(rows):
-            return rows.rearrange("p t (c i) -> p c t i", i=2)
+            return rows.rearrange("p t (c i) -> p c t i", i=4)
 
         def fetch_first(c, t):
             if c == 0 and t < 2:
@@ -183,7 +187,7 @@ def tile_picked_yhopsum_max_po_kernel(
                 nc.scalar.activation(first[c][:, t, :], y[t][:].indirect(entries(s1_t, c)), ACT.Copy)
 
         def scalar_fetches_second(c, t):
-            return c == last or (c, t) == (last - 1, PACK - 1)
+            return c == last or (c == last - 1 and t >= SHARED_FROM)
 
         def fetch_second(c, t):
             nc.scalar.activation(middle[c, t], y[t][:].indirect(entries(s2_t, c)), ACT.Copy)
@@ -252,9 +256,14 @@ def tile_picked_yhopsum_max_po_kernel(
 
         def hand_on(c):
             cols = slice(starts[c], starts[c] + CHUNKS[c])
-            out_words = held([P, CHUNKS[c]], U32, "out_words%d" % c, {0: "path3", 1: "hid3"}.get(c))
-            nc.vector.quantize_mx(out=out_words[:].bitcast(FP8X4), scales=out_scales[:, cols], in_=rounded[c][:])
-            nc.sync.dma_start(out=out_words_hbm[:, cols], in_=out_words[:].bitcast(I32))
+            group = [g for g in STORE_GROUPS if c in g][0]
+            begin, end = starts[group[0]], starts[group[-1]] + CHUNKS[group[-1]]
+            if c == group[0]:
+                out_words[group] = held([P, end - begin], U32, "out_words%d" % c, {0: "path3", 1: "hid3"}.get(c))
+            words = out_words[group][:, cols.start - begin : cols.stop - begin]
+            nc.vector.quantize_mx(out=words.bitcast(FP8X4), scales=out_scales[:, cols], in_=rounded[c][:])
+            if c == group[-1]:
+                nc.sync.dma_start(out=out_words_hbm[:, begin:end], in_=out_words[group][:].bitcast(I32))
 
         def hidden_steps(c):
             return [lambda: take_larger(c), lambda: give_sign(c), lambda: multiply(c), lambda: None]
@@ -267,7 +276,6 @@ def tile_picked_yhopsum_max_po_kernel(
             add_second(0, t)
         for t in range(PACK):
             fetch_sink(0, t)
-        w2s = deal_scales(w2s_raw, 1, "w2s")
         add_third(0, PACK - 1)
         for t in range(PACK):
             fetch_first(1, t)
@@ -281,28 +289,32 @@ def tile_picked_yhopsum_max_po_kernel(
         empty_banks(0)
         round_result(0)
         wide, narrow = CHUNKS[last - 1], CHUNKS[last]
-        late = held([P, (PACK + 1) * wide + 3 * PACK * narrow], F32, "late", "hid_words0")
-        middle[last - 1, PACK - 1] = late[:, :wide]
-        at = wide
-        for table, c in ((sink, last - 1), (first, last), (sink, last)):
+        late = held([P, (2 * PACK - SHARED_FROM) * wide + 2 * PACK * narrow], F32, "late", "hid_words0")
+        at = 0
+        for t in range(SHARED_FROM, PACK):
+            middle[last - 1, t] = late[:, at : at + wide]
+            at = at + wide
+        for table, c in ((sink, last - 1), (first, last)):
             table[c] = late[:, at : at + PACK * CHUNKS[c]].rearrange("p (t r) -> p t r", t=PACK)
             at = at + PACK * CHUNKS[c]
         for t in range(PACK):
             middle[last, t] = late[:, at + t * narrow : at + (t + 1) * narrow]
-        fetch_second(2, PACK - 1)
+        for t in range(SHARED_FROM, PACK):
+            fetch_second(2, t)
         for t in range(PACK):
             fetch_sink(2, t)
         for t in range(PACK):
             fetch_first(3, t)
             fetch_second(3, t)
         for t in range(PACK):
-            fetch_sink(3, t)
-        for t in range(PACK):
             add_third(1, t)
         for t, step in enumerate(hidden_steps(1)):
             add_second(2, t)
             step()
         empty_banks(1)
+        sink[last] = held([P, PACK, narrow], F32, "sink_last", "hid_words1")[:]
+        for t in range(PACK):
+            fetch_sink(3, t)
         round_result(1)
         for t in range(PACK):
             add_third(2, t)

from contextlib import ExitStack

import concourse.mybir as mybir

K, T, S, N, H, U = 1024, 1024, 512, 512, 512, 1024
FLOPS = 2 * K * N * S + 2 * H * N * U

F32 = mybir.dt.float32
BF16 = mybir.dt.bfloat16
I32 = mybir.dt.int32
U32 = mybir.dt.uint32
U16 = mybir.dt.uint16
U8 = mybir.dt.uint8
FP8X4 = mybir.dt.float8_e4m3fn_x4
FP4X4 = mybir.dt.float4_e2m1fn_x4
ALU = mybir.AluOpType
ACT = mybir.ActivationFunctionType

P = 128
PACK = 4
PASSES = K // (P * PACK)
STRIPE = 16
BANK = 512
SIGN_RUN = 64
CHUNKS = (256, 384, 256, 128)
STORE_GROUPS = ((0,), (1, 2), (3,))
SHARED_FROM = 2


def tile_picked_yhopsum_max_po_kernel(
    tc, x_words, x_scales, w1_words, w1_scales, unit, w2_words, w2_scales, offs, s1, s2, s3, sk, out_0, out_1, out_2
):
    nc = tc.nc
    with ExitStack() as ctx:
        keep = ctx.enter_context(tc.tile_pool(name="keep", bufs=1))
        psum = ctx.enter_context(tc.psum_pool(name="psum", bufs=1))

        def held(shape, dtype, name, tag=None):
            return keep.tile(shape, dtype, name=name, tag=tag or name, align_bytes=64)

        def load_scale_rows(queue, dst, src):
            for q in range(4):
                queue.dma_start(
                    out=dst[32 * q : 32 * q + 4].bitcast(I32),
                    in_=src[:, 4 * q : 4 * q + 4, :].rearrange("o r c -> r o c").bitcast(I32),
                )

        def load_list(src, name):
            tile_ = keep.tile(list(src.shape), U16, name=name)
            nc.sync.dma_start(tile_[:], src)
            return tile_

        xs_raw = held([P, T], U8, "xs_raw", "xs_then_w2w")
        w1s_raw = held([P, PASSES, N], U8, "w1s_raw")
        xs_second = held([P, S], U8, "xs_second")
        nc.vector.memset(xs_raw[:].bitcast(I32), 0)
        nc.vector.memset(w1s_raw[:].bitcast(I32), 0)
        nc.vector.memset(xs_second[:].bitcast(I32), 0)

        xw_raw = [held([P, T], U32, "xw_raw%d" % o) for o in range(PASSES)]

        def load_x_words(o):
            nc.sync.dma_start(out=xw_raw[o][:].bitcast(I32), in_=x_words[o].rearrange("p c r -> p (c r)").bitcast(I32))

        w1w_raw = held([P, PASSES, 2 * N], U8, "w1w_raw")
        nc.sync.dma_start(out=w1w_raw[:].bitcast(I32), in_=w1_words.rearrange("o p c -> p o c").bitcast(I32))
        for q in range(4):
            nc.sync.dma_start(
                out=xs_raw[32 * q : 32 * q + 4 * PASSES].bitcast(I32), in_=x_scales[:, 4 * q : 4 * q + 4, :].bitcast(I32)
            )
        offs_t = load_list(offs, "offs_t")
        load_x_words(0)
        load_scale_rows(nc.sync, w1s_raw, w1_scales)
        load_x_words(1)
        unit_t = held([P, PACK], F32, "unit_t")
        nc.sync.dma_start(out=unit_t[:], in_=unit.rearrange("(p t) o -> p (t o)", t=PACK))
        s1_t = load_list(s1, "s1_t")
        sk_t = load_list(sk, "sk_t")
        s2_t = load_list(s2, "s2_t")
        s3_t = load_list(s3, "s3_t")

        def deal_words(dealt, raw):
            nc.vector.tensor_copy(
                out=dealt.rearrange("p t (m b) -> p t m b", b=2),
                in_=raw.rearrange("p (m t b) -> p t m b", t=PACK, b=2),
            )

        def deal_scales(raw, passes, name):
            dealt = held([P, passes, PACK, P], U8, name)
            nc.vector.tensor_copy(out=dealt[:], in_=raw[:].rearrange("p o (m t) -> p o t m", t=PACK))
            return dealt

        xs_first = held([P, S], U8, "xs_first")
        nc.vector.tensor_copy(xs_first[:], xs_raw[:].indirect(offs_t[:]))
        for q in range(4):
            nc.scalar.dma_start(
                out=xs_second[32 * q : 32 * q + 4].bitcast(I32), in_=xs_first[32 * q + 4 : 32 * q + 8].bitcast(I32)
            )
        xs = [xs_first, xs_second]
        w2_raw = held([P, 3, N], U8, "w2_raw", "xs_then_w2w")
        w2w_raw = w2_raw[:, 0:2, :].rearrange("p a c -> p (a c)")
        w2s_raw = w2_raw[:, 2:3, :]
        nc.sync.dma_start(out=w2w_raw.bitcast(I32), in_=w2_words[0].bitcast(I32))
        nc.gpsimd.memset(w2s_raw.bitcast(I32), 0)
        load_scale_rows(nc.sync, w2s_raw, w2_scales)

        xw = [held([P, S], U32, "xw0")]
        w1w = [held([P, PACK, 2 * P], U8, "w1w0")]
        deal_words(w1w[0][:], w1w_raw[:, 0, :])
        nc.vector.tensor_copy(xw[0][:], xw_raw[0][:].indirect(offs_t[:]))
        w1s = deal_scales(w1s_raw, PASSES, "w1s")
        w1w.append(held([P, PACK, 2 * P], U8, "w1w1", "w1s_raw"))
        deal_words(w1w[1][:], w1w_raw[:, 1, :])
        xw.append(held([P, S], U32, "xw1", "w1w_raw"))
        halves = [slice(h * S // 2, (h + 1) * S // 2) for h in range(2)]
        for cols in halves:
            picks = offs_t[:, cols.start // STRIPE : cols.stop // STRIPE]
            nc.vector.tensor_copy(xw[1][:, cols], xw_raw[1][:].indirect(picks))

        size = held([P, PACK], F32, "size")
        nc.scalar.activation(size[:], unit_t[:], ACT.Abs)
        sign = held([P, SIGN_RUN // PACK, PACK], BF16, "sign")
        nc.scalar.activation(
            sign[:], unit_t[:].unsqueeze(1).to_broadcast([P, SIGN_RUN // PACK, PACK]), ACT.Sign
        )

        def new_bank(shape):
            return psum.tile(shape, F32, name="bank", tag="bank", bufs=8)

        spans = [halves] + [[slice(0, S)]] * (PACK - 1)
        y_banks = [[new_bank([P, cols.stop - cols.start]) for cols in spans[t]] for t in range(PACK)]

        def first_product(t, o):
            for bank, cols in zip(y_banks[t], spans[t]):
                nc.tensor.matmul_mx(
                    out=bank[:],
                    lhsT=w1w[o][:, t, :].bitcast(FP4X4),
                    lhsT_scale=w1s[:, o, t, :],
                    rhs=xw[o][:, cols].bitcast(FP8X4),
                    rhs_scale=xs[o][:, cols],
                    start=(o == 0),
                    stop=(o == PASSES - 1),
                )

        for pair in range(PACK // 2):
            for o in range(PASSES):
                for t in (2 * pair, 2 * pair + 1):
                    first_product(t, o)
        w2w = held([P, PACK, 2 * P], U8, "w2w")
        deal_words(w2w[:], w2w_raw)
        w2s = deal_scales(w2s_raw, 1, "w2s")
        y = [held([P, S], F32, "y%d" % t) for t in range(PACK)]

        def scale_rows(t):
            for bank, cols in zip(y_banks[t], spans[t]):
                nc.scalar.activation(y[t][:, cols], bank[:], ACT.Copy, scale=size[:, t : t + 1])

        last = len(CHUNKS) - 1
        starts = [sum(CHUNKS[:c]) for c in range(len(CHUNKS))]
        second = [held([P, PACK, n], F32, "second%d" % c) for c, n in enumerate(CHUNKS)]
        path = [held([P, PACK, n], F32, "path%d" % c) for c, n in enumerate(CHUNKS)]
        larger = [held([P, PACK * n], BF16, "larger%d" % c) for c, n in enumerate(CHUNKS)]
        hid = [held([P, PACK * n], BF16, "hid%d" % c) for c, n in enumerate(CHUNKS)]
        hid_scales = [held([P, n], U8, "hid_scales%d" % c) for c, n in enumerate(CHUNKS)]
        result = [held([P, PACK, n], F32, "result%d" % c) for c, n in enumerate(CHUNKS)]
        rounded, out_words = {}, {}
        out_scales = held([P, U], U8, "out_scales")
        out_rows = out_0.rearrange("(p t) r -> p t r", t=PACK)
        out_words_hbm = out_1[0].rearrange("p c r -> p (c r)").bitcast(I32)
        first = {c: held([P, PACK, CHUNKS[c]], F32, "first%d" % c)[:] for c in range(last)}
        sink = {c: held([P, PACK, CHUNKS[c]], F32, "sink%d" % c)[:] for c in range(last - 1)}
        middle, hid_words, banks = {}, {}, {}

        def entries(list_tile, c):
            return list_tile[:, starts[c] // STRIPE : (starts[c] + CHUNKS[c]) // STRIPE]

        def woven(flat):
            return flat.rearrange("p (c i t) -> p c t i", i=4, t=PACK)

        def planes(rows):
            return rows.rearrange("p t (c i) -> p c t i", i=4)

        def fetch_first(c, t):
            if c == 0 and t < 2:
                nc.vector.tensor_copy(first[c][:, t, :], y[t][:].indirect(entries(s1_t, c)))
            else:
                nc.scalar.activation(first[c][:, t, :], y[t][:].indirect(entries(s1_t, c)), ACT.Copy)

        def scalar_fetches_second(c, t):
            return c == last or (c == last - 1 and t >= SHARED_FROM)

        def fetch_second(c, t):
            nc.scalar.activation(middle[c, t], y[t][:].indirect(entries(s2_t, c)), ACT.Copy)

        def fetch_sink(c, t):
            nc.scalar.activation(sink[c][:, t, :], y[t][:].indirect(entries(sk_t, c)), ACT.Copy, scale=1.5)

        def add_second(c, t):
            other = middle[c, t] if scalar_fetches_second(c, t) else y[t][:].indirect(entries(s2_t, c))
            nc.vector.tensor_tensor(second[c][:, t, :], other, first[c][:, t, :], ALU.add)

        def add_third(c, t):
            nc.vector.tensor_tensor(path[c][:, t, :], y[t][:].indirect(entries(s3_t, c)), second[c][:, t, :], ALU.add)

        def take_larger(c):
            nc.vector.tensor_tensor(woven(larger[c][:]), planes(path[c][:]), planes(sink[c]), ALU.max)

        def give_sign(c):
            runs = PACK * CHUNKS[c] // SIGN_RUN
            nc.vector.tensor_tensor(
                hid[c][:].rearrange("p (a b) -> p a b", b=SIGN_RUN),
                larger[c][:].rearrange("p (a b) -> p a b", b=SIGN_RUN),
                sign[:].rearrange("p a t -> p (a t)").unsqueeze(1).to_broadcast([P, runs, SIGN_RUN]),
                ALU.mult,
            )

        def blocks(c):
            found, at = [], 0
            while at < CHUNKS[c]:
                width = 2 * P if CHUNKS[c] - at >= 2 * P else P
                found.append((at, width))
                at = at + width
            return found

        def multiply(c):
            hid_words[c] = held([P, CHUNKS[c]], U32, "hid_words%d" % c)
            nc.vector.quantize_mx(out=hid_words[c][:].bitcast(FP8X4), scales=hid_scales[c][:], in_=hid[c][:])
            banks[c] = []
            for at, width in blocks(c):
                per_bank = 2 if c == last else BANK // width
                for t0 in range(0, PACK, per_bank):
                    bank = new_bank([P, per_bank, width])
                    for j in range(per_bank):
                        nc.tensor.matmul_mx(
                            out=bank[:, j, :],
                            lhsT=w2w[:, t0 + j, :].bitcast(FP4X4),
                            lhsT_scale=w2s[:, 0, t0 + j, :],
                            rhs=hid_words[c][:, at : at + width].bitcast(FP8X4),
                            rhs_scale=hid_scales[c][:, at : at + width],
                            start=True,
                            stop=True,
                        )
                    banks[c].append((bank, result[c][:, t0 : t0 + per_bank, at : at + width]))

        def empty_banks(c):
            for bank, place in banks[c]:
                nc.scalar.copy(place, bank[:])
            nc.sync.dma_start(out=out_rows[:, :, starts[c] : starts[c] + CHUNKS[c]], in_=result[c][:])

        def round_result(c):
            rounded[c] = held([P, PACK * CHUNKS[c]], BF16, "rounded%d" % c, "rounded1" if c == last - 1 else None)
            if c >= last - 1:
                nc.vector.tensor_copy(woven(rounded[c][:]), planes(result[c][:]))
            else:
                nc.scalar.copy(woven(rounded[c][:]), planes(result[c][:]))

        def hand_on(c):
            cols = slice(starts[c], starts[c] + CHUNKS[c])
            group = [g for g in STORE_GROUPS if c in g][0]
            begin, end = starts[group[0]], starts[group[-1]] + CHUNKS[group[-1]]
            if c == group[0]:
                out_words[group] = held([P, end - begin], U32, "out_words%d" % c, {0: "path3", 1: "hid3"}.get(c))
            words = out_words[group][:, cols.start - begin : cols.stop - begin]
            nc.vector.quantize_mx(out=words.bitcast(FP8X4), scales=out_scales[:, cols], in_=rounded[c][:])
            if c == group[-1]:
                nc.sync.dma_start(out=out_words_hbm[:, begin:end], in_=out_words[group][:].bitcast(I32))

        def hidden_steps(c):
            return [lambda: take_larger(c), lambda: give_sign(c), lambda: multiply(c), lambda: None]

        for t in range(PACK):
            scale_rows(t)
            fetch_first(0, t)
            if t >= 1:
                add_third(0, t - 1)
            add_second(0, t)
        for t in range(PACK):
            fetch_sink(0, t)
        add_third(0, PACK - 1)
        for t in range(PACK):
            fetch_first(1, t)
        for t in range(PACK):
            fetch_sink(1, t)
        for t in range(PACK):
            fetch_first(2, t)
        for t, step in enumerate(hidden_steps(0)):
            add_second(1, t)
            step()
        empty_banks(0)
        round_result(0)
        wide, narrow = CHUNKS[last - 1], CHUNKS[last]
        late = held([P, (2 * PACK - SHARED_FROM) * wide + 2 * PACK * narrow], F32, "late", "hid_words0")
        at = 0
        for t in range(SHARED_FROM, PACK):
            middle[last - 1, t] = late[:, at : at + wide]
            at = at + wide
        for table, c in ((sink, last - 1), (first, last)):
            table[c] = late[:, at : at + PACK * CHUNKS[c]].rearrange("p (t r) -> p t r", t=PACK)
            at = at + PACK * CHUNKS[c]
        for t in range(PACK):
            middle[last, t] = late[:, at + t * narrow : at + (t + 1) * narrow]
        for t in range(SHARED_FROM, PACK):
            fetch_second(2, t)
        for t in range(PACK):
            fetch_sink(2, t)
        for t in range(PACK):
            fetch_first(3, t)
            fetch_second(3, t)
        for t in range(PACK):
            add_third(1, t)
        for t, step in enumerate(hidden_steps(1)):
            add_second(2, t)
            step()
        empty_banks(1)
        sink[last] = held([P, PACK, narrow], F32, "sink_last", "hid_words1")[:]
        for t in range(PACK):
            fetch_sink(3, t)
        round_result(1)
        for t in range(PACK):
            add_third(2, t)
        for t, step in enumerate(hidden_steps(2)):
            add_second(3, t)
            step()
        empty_banks(2)
        for t in range(PACK):
            add_third(3, t)
        take_larger(3)
        hand_on(0)
        give_sign(3)
        multiply(3)
        empty_banks(3)
        hand_on(1)
        round_result(2)
        hand_on(2)
        round_result(3)
        hand_on(3)
        for q in range(4):
            queue = nc.sync if q % 2 == 0 else nc.scalar
            queue.dma_start(
                out=out_2[0, 4 * q : 4 * q + 4, :].bitcast(I32), in_=out_scales[32 * q : 32 * q + 4, :].bitcast(I32)
            )
